import numpy as np
import ml_dtypes


def mxq(x, axis, fmt="e4m3"):
    dtype, down = {"e4m3": (ml_dtypes.float8_e4m3fn, 7), "e5m2": (ml_dtypes.float8_e5m2, 14)}[fmt]
    v = np.moveaxis(np.asarray(x, np.float32).astype(ml_dtypes.bfloat16).astype(np.float64), axis, -1)
    blocks = v.reshape(v.shape[:-1] + (-1, 32))
    amax = np.abs(blocks).max(-1, keepdims=True)
    byte = np.maximum(np.where(amax > 0, np.frexp(amax)[1] - 1 + 127, 0) - down, 1)
    scale = np.exp2(byte - 127.0)
    codes = (blocks / scale).astype(np.float32).astype(dtype).astype(np.float64)
    return np.moveaxis((codes * scale).reshape(v.shape), -1, axis)


WIDE = False


def mx_kscale(k):
    if not WIDE:
        return np.ones(k)
    levels = np.array([10, -10, 5, -5, 0])
    if k % 512:
        return np.exp2(np.random.permutation(np.resize(levels, k // 32))).repeat(32)
    a = np.empty((k // 512, 16))
    for p in range(k // 512):
        a[p, :8] = np.random.permutation(np.resize(levels, 8))
        for g in range(8):
            far = levels[np.abs(levels - a[p, g]) >= 10]
            a[p, g + 8] = far[np.random.randint(len(far))]
    return np.exp2(a.ravel()).repeat(32)


BF16 = ml_dtypes.bfloat16


def bf(x):
    return np.asarray(x, np.float32).astype(BF16)


def f64(x):
    return np.asarray(x).astype(np.float64)


V, D, H, F = 1024, 1024, 2, 512

EPS = 1e-5
SLOPE = 0.2


def leaky(z):
    return np.maximum(z, SLOPE * z)


def draw0():
    s, t = mx_kscale(D), mx_kscale(H * F)
    return {"x": bf(np.random.standard_normal((V, D)) * s),
            "wq": bf(np.random.standard_normal((D, H * F)) / np.sqrt(D) / s[:, None]),
            "bq": bf(0.3 * np.random.standard_normal(H * F)),
            "gq": bf((1.0 + 0.1 * np.random.standard_normal(H * F)) * t),
            "wk": bf(np.random.standard_normal((D, H * F)) / np.sqrt(D) / s[:, None] / t),
            "bk": bf(0.3 * np.random.standard_normal(H * F) / t),
            "edge": bf(np.random.uniform(0.1, 1.9, (H, V, V)))}


def core(x, wq, bq, gq, wk, bk, edge):
    nodes = mxq(f64(x), 1, "e4m3")
    q = (nodes @ mxq(f64(wq), 0, "e4m3")) + f64(bq)
    q = q.reshape(V, H, F)
    q = q / np.sqrt(np.mean(q * q, axis=2, keepdims=True) + EPS)
    q = q.reshape(V, H * F) * f64(gq)
    k = leaky((nodes @ mxq(f64(wk), 0, "e4m3")) + f64(bk))
    e = f64(edge)
    lift = np.zeros((V, V))
    for h in range(H):
        cols = slice(h * F, (h + 1) * F)
        z = mxq(q[:, cols], 1, "e4m3") @ mxq(k[:, cols], 1, "e4m3").T
        z = leaky(z / np.sqrt(F))
        p = e[h] * np.exp(z - np.max(z, axis=1, keepdims=True))
        p = p / np.sum(p, axis=1, keepdims=True)
        lift = lift + p * (V / H)
    return lift


def e4m3fn_bytes(y):
    return np.clip(np.asarray(y, np.float64), -448.0, 448.0).astype(np.float32).astype(ml_dtypes.float8_e4m3fn).view(np.uint8)


def e4m3fn_values(b):
    return np.asarray(b, np.uint8).view(ml_dtypes.float8_e4m3fn).astype(np.float64)


def setup_inputs():
    d = draw0()
    x0 = np.asarray(d['x']).astype(np.float64)
    s = (np.max(np.abs(x0), axis=(0,), keepdims=True) / 448.0).astype(np.float32)
    out = {}
    for k, v in d.items():
        if k == 'x':
            out['x_bytes'] = e4m3fn_bytes(x0 / s.astype(np.float64))
            out['x_scale'] = s
        else:
            out[k] = v
    return out


def reference(x_bytes, x_scale, wq, bq, gq, wk, bk, edge):
    return core(e4m3fn_values(x_bytes) * x_scale.astype(np.float64), wq, bq, gq, wk, bk, edge)

from contextlib import ExitStack

import concourse.mybir as mybir
from concourse.masks import make_identity

V, D, H, F = 1024, 1024, 2, 512
HF = H * F
EPS = 1e-5
SLOPE = 0.2
FLOPS = 2 * V * D * HF * 2 + 2 * H * V * V * F

F32 = mybir.dt.float32
BF16 = mybir.dt.bfloat16
U32 = mybir.dt.uint32
U8 = mybir.dt.uint8
FP8 = mybir.dt.float8_e4m3fn
FP8X4 = mybir.dt.float8_e4m3fn_x4
ACT = mybir.ActivationFunctionType
ALU = mybir.AluOpType

P = 128
T = 4
G = D // (P * T)
A = V // P
C = V // 512
SCALE = 1.0 / (F ** 0.5)


def tile_graph_attention_lift_f5_kernel(tc, x_bytes, x_scale, wq, bq, gq, wk, bk, edge, out):
    nc = tc.nc
    with ExitStack() as ctx:
        keep = ctx.enter_context(tc.tile_pool(name="keep", bufs=1))
        work = ctx.enter_context(tc.tile_pool(name="work", bufs=2))
        psum = ctx.enter_context(tc.psum_pool(name="psum", bufs=8))

        sc = keep.tile([P, D], F32, name="sc")
        nc.scalar.dma_start(out=sc[:], in_=x_scale.rearrange("o k -> (o k)").partition_broadcast(P))
        xb, wraw, eb = {}, {}, {}

        def load_x(a):
            xb[a] = work.tile([P, D], U8, name="xb", bufs=8)
            nc.sync.dma_start(out=xb[a][:], in_=x_bytes[a * P : (a + 1) * P, :])

        def load_w(nm, h):
            w = wq if nm == "q" else wk
            for g in range(G):
                wt = work.tile([P, T, F], BF16, name="raw", bufs=6)
                nc.sync.dma_start(
                    out=wt[:],
                    in_=w[g * 512 : (g + 1) * 512, h * F : (h + 1) * F].rearrange("(p j) n -> p j n", j=T),
                )
                wraw[nm, h, g] = wt

        def load_e(h, i):
            eb[h, i] = work.tile([P, V], BF16, name="eb", bufs=7)
            nc.sync.dma_start(out=eb[h, i][:], in_=edge[h, i * P : (i + 1) * P, :])

        load_x(0)
        load_x(1)
        bqt = keep.tile([P, H, T], BF16, name="bqt")
        gqt = keep.tile([P, H, T], BF16, name="gqt")
        bkt = keep.tile([P, H, T], BF16, name="bkt")
        for tl, v in ((bqt, bq), (gqt, gq), (bkt, bk)):
            nc.gpsimd.dma_start(out=tl[:], in_=v.rearrange("(h p t) -> p h t", h=H, t=T))
        for a in range(2, 5):
            load_x(a)
        load_w("q", 0)
        load_w("k", 0)
        for a in range(5, A):
            load_x(a)

        ident = keep.tile([P, P], F32, name="ident")
        make_identity(nc, ident[:])
        ones = keep.tile([P, P], F32, name="ones")
        nc.gpsimd.memset(ones[:], 1.0)
        g32 = keep.tile([P, H, T], F32, name="g32")
        gb = keep.tile([P, H, T], F32, name="gb")

        def small():
            nc.vector.tensor_copy(out=g32[:], in_=gqt[:])
            nc.vector.tensor_tensor(out=gb[:], in0=gqt[:], in1=bqt[:], op=ALU.mult)

        xg = keep.tile([P, G, V, T], BF16, name="xg", align_bytes=64)
        xq = keep.tile([P, G, V], U32, name="xq", align_bytes=64)
        xs = keep.tile([P, G, V], U8, name="xs", align_bytes=64)

        def quantize(codes, scales, src):
            nc.vector.quantize_mx(out=codes.bitcast(FP8X4), scales=scales, in_=src.rearrange("p n t -> p (n t)"))

        xv, xt = {}, {}

        def x_product(a):
            xv[a] = work.tile([P, D], BF16, name="xv")
            nc.vector.tensor_tensor(out=xv[a][:], in0=xb[a][:].bitcast(FP8), in1=sc[:], op=ALU.mult)

        def x_turn(a):
            words = xv[a][:].bitcast(F32)
            xt[a] = psum.tile([P, G, 2, P], F32, name="sc", bufs=4)
            for g in range(G):
                for u in range(2):
                    nc.tensor.transpose(xt[a][:, g, u, :], words[:, 256 * g + u : 256 * (g + 1) : 2], ident[:])

        def x_copy(a):
            nc.scalar.copy(
                out=xg[:, :, a * P : (a + 1) * P, :].bitcast(F32),
                in_=xt[a][:].rearrange("p g u r -> p g r u"),
            )

        def x_quant(c, g):
            cols = slice(c * 512, (c + 1) * 512)
            quantize(xq[:, g, cols], xs[:, g, cols], xg[:, g, cols, :])

        wcode, wscale, wg = {}, {}, {}
        for h in range(H):
            for nm in ("q", "k"):
                wcode[nm, h] = keep.tile([P, G, F], U32, name=f"wc{nm}{h}", align_bytes=64)
                wscale[nm, h] = keep.tile([P, G, F], U8, name=f"ws{nm}{h}", align_bytes=64)

        def w_inter(nm, h, g, eng):
            wg[nm, h, g] = work.tile([P, F, T], BF16, name="wg", bufs=2, align_bytes=64)
            o = wg[nm, h, g][:].rearrange("p (t m) j -> p t m j", t=T)
            i = wraw[nm, h, g][:].rearrange("p j (m t) -> p t m j", t=T)
            if eng == "S":
                nc.scalar.copy(out=o, in_=i)
            else:
                nc.vector.tensor_copy(out=o, in_=i)

        def w_quant(nm, h, g):
            quantize(wcode[nm, h][:, g, :], wscale[nm, h][:, g, :], wg[nm, h, g][:])

        def project(ps, nm, h, t, c):
            for g in range(G):
                nc.tensor.matmul_mx(
                    out=ps[:],
                    lhsT=wcode[nm, h][:, g, t * P : (t + 1) * P].bitcast(FP8X4),
                    lhsT_scale=wscale[nm, h][:, g, t * P : (t + 1) * P],
                    rhs=xq[:, g, c * 512 : (c + 1) * 512].bitcast(FP8X4),
                    rhs_scale=xs[:, g, c * 512 : (c + 1) * 512],
                    start=(g == 0),
                    stop=(g == G - 1),
                )

        qcode = [keep.tile([P, V], U32, name=f"qcode{h}", align_bytes=64) for h in range(H)]
        qscale = [keep.tile([P, V], U8, name=f"qscale{h}", align_bytes=64) for h in range(H)]
        kcode = [keep.tile([P, V], U32, name=f"kcode{h}", align_bytes=64) for h in range(H)]
        kscale = [keep.tile([P, V], U8, name=f"kscale{h}", align_bytes=64) for h in range(H)]
        ys, sqs, rs, bs, nss, prj = {}, {}, {}, {}, {}, {}

        def q_mm(h, c, t):
            ps = psum.tile([P, 512], F32, name="ps", bufs=2)
            project(ps, "q", h, t, c)
            prj["q", h, c, t] = ps

        def q_sq(h, c, t):
            if t == 0:
                sqs[h, c] = work.tile([P, T, 512], F32, name="sq")
            nc.scalar.activation(out=sqs[h, c][:, t, :], in_=prj["q", h, c, t][:], func=ACT.Square, bias=bqt[:, h, t : t + 1])

        def q_aff(h, c, t):
            if t == 0:
                ys["q", h, c] = work.tile([P, T, 512], F32, name="y", bufs=3)
            nc.scalar.activation(
                out=ys["q", h, c][:, t, :], in_=prj["q", h, c, t][:], func=ACT.Identity,
                bias=gb[:, h, t : t + 1], scale=g32[:, h, t : t + 1],
            )

        def q_sum(h, c, t):
            if t == 0:
                nss[h, c] = psum.tile([P, 512], F32, name="ns", bufs=2)
            nc.tensor.matmul(out=nss[h, c][:], lhsT=ones[:], rhs=sqs[h, c][:, t, :], start=(t == 0), stop=(t == T - 1))

        def q_root(h, c):
            rs[h, c] = work.tile([P, 512, 1], F32, name="r")
            nc.scalar.activation(out=rs[h, c][:, :, 0], in_=nss[h, c][:], func=ACT.Abs_reciprocal_sqrt, scale=1.0 / F, bias=EPS)

        def q_norm(h, c):
            bs["q", h, c] = work.tile([P, 512, T], BF16, name="qb", align_bytes=64)
            nc.vector.tensor_tensor(
                out=bs["q", h, c][:], in0=ys["q", h, c][:].rearrange("p t n -> p n t"),
                in1=rs[h, c][:].to_broadcast([P, 512, T]), op=ALU.mult,
            )

        def q_quant(h, c):
            cols = slice(c * 512, (c + 1) * 512)
            quantize(qcode[h][:, cols], qscale[h][:, cols], bs["q", h, c][:])

        def k_mm(h, c, t):
            ps = psum.tile([P, 512], F32, name="ps", bufs=2)
            project(ps, "k", h, t, c)
            prj["k", h, c, t] = ps

        def k_aff(h, c, t):
            if t == 0:
                ys["k", h, c] = work.tile([P, T, 512], F32, name="y", bufs=3)
            nc.scalar.activation(out=ys["k", h, c][:, t, :], in_=prj["k", h, c, t][:], func=ACT.Identity, bias=bkt[:, h, t : t + 1])

        def k_leaky(h, c):
            bs["k", h, c] = work.tile([P, 512, T], BF16, name="kb", align_bytes=64)
            yv = ys["k", h, c][:].rearrange("p t n -> p n t")
            nc.vector.scalar_tensor_tensor(out=bs["k", h, c][:], in0=yv, scalar=SLOPE, in1=yv, op0=ALU.mult, op1=ALU.max)

        def k_quant(h, c):
            cols = slice(c * 512, (c + 1) * 512)
            quantize(kcode[h][:, cols], kscale[h][:, cols], bs["k", h, c][:])

        mx = keep.tile([P, H, A, 2], F32, name="mx")
        nm1 = keep.tile([P, H, A], F32, name="nm1")
        nmx = keep.tile([P, H, A], F32, name="nmx")
        ssum = keep.tile([P, A, H], F32, name="ssum")
        rec = keep.tile([P, A, H], F32, name="rec")
        fac = keep.tile([P, A, H], F32, name="fac")
        zt, pss = {}, {}

        def s_mm(h, i):
            for c in range(C):
                ps = psum.tile([P, 512], F32, name="sc", bufs=4)
                nc.tensor.matmul_mx(
                    out=ps[:],
                    lhsT=qcode[h][:, i * P : (i + 1) * P].bitcast(FP8X4),
                    lhsT_scale=qscale[h][:, i * P : (i + 1) * P],
                    rhs=kcode[h][:, c * 512 : (c + 1) * 512].bitcast(FP8X4),
                    rhs_scale=kscale[h][:, c * 512 : (c + 1) * 512],
                    start=True,
                    stop=True,
                )
                pss[h, i, c] = ps

        def s_max(h, i):
            zt[h, i] = work.tile([P, V], F32, name=f"z{h}", bufs=8 if h == 0 else 4)
            for c in range(C):
                nc.vector.tensor_scalar(
                    out=zt[h, i][:, c * 512 : (c + 1) * 512],
                    in0=pss[h, i, c][:],
                    scalar1=SLOPE * SCALE,
                    scalar2=None,
                    op0=ALU.mult,
                    op1=ALU.max,
                    accum_out=mx[:, h, i, c : c + 1],
                )
            nc.gpsimd.tensor_scalar(
                out=nm1[:, h, i : i + 1],
                in0=mx[:, h, i, 0:1],
                scalar1=mx[:, h, i, 1:2],
                scalar2=-1.0,
                op0=ALU.max,
                op1=ALU.mult,
            )
            nc.gpsimd.tensor_scalar(
                out=nmx[:, h, i : i + 1],
                in0=nm1[:, h, i : i + 1],
                scalar1=1.0 / SLOPE,
                scalar2=nm1[:, h, i : i + 1],
                op0=ALU.mult,
                op1=ALU.min,
            )

        def s_leaky(h, i):
            for c in range(C):
                zc = zt[h, i][:, c * 512 : (c + 1) * 512]
                nc.vector.scalar_tensor_tensor(
                    out=zc, in0=pss[h, i, c][:], scalar=SCALE, in1=zc, op0=ALU.mult, op1=ALU.max
                )

        def s_exp(h, i):
            z = zt[h, i]
            nc.scalar.activation(out=z[:], in_=z[:], func=ACT.Exp, bias=nmx[:, h, i : i + 1])

        def s_edge(h, i):
            z = zt[h, i]
            nc.vector.scalar_tensor_tensor(
                out=z[:], in0=z[:], scalar=1.0, in1=eb[h, i][:], op0=ALU.mult, op1=ALU.mult,
                accum_out=ssum[:, i, h : h + 1],
            )
            n = h * A + i + 7
            if n < H * A:
                load_e(n // A, n % A)

        def c_fac(i):
            nc.vector.reciprocal(out=rec[:, i, :], in_=ssum[:, i, :])
            nc.gpsimd.tensor_scalar(
                out=fac[:, i, :], in0=rec[:, i, :], scalar1=float(V // H), scalar2=0.0, op0=ALU.mult, op1=ALU.add
            )

        def c_scale(i):
            nc.scalar.activation(out=zt[0, i][:], in_=zt[0, i][:], func=ACT.Copy, scale=fac[:, i, 0:1])

        def c_add(i):
            nc.vector.scalar_tensor_tensor(
                out=zt[0, i][:], in0=zt[1, i][:], scalar=fac[:, i, 1:2], in1=zt[0, i][:], op0=ALU.mult, op1=ALU.add
            )
            nc.sync.dma_start(out=out[i * P : (i + 1) * P, :], in_=zt[0, i][:])

        def x_tile(a):
            x_product(a)
            x_turn(a)
            x_copy(a)

        def q_mms(h, c):
            for t in range(T):
                q_mm(h, c, t)

        def q_sums(h, c):
            for t in range(T):
                q_sum(h, c, t)

        def k_mms(h, c):
            for t in range(T):
                k_mm(h, c, t)

        def k_affs(h, c):
            for t in range(T):
                k_aff(h, c, t)

        def q_affs(h, c, t0=0, t1=T):
            for t in range(t0, t1):
                q_sq(h, c, t)
                q_aff(h, c, t)

        def q_finish(h, c):
            q_norm(h, c)
            q_quant(h, c)

        def k_finish(h, c):
            k_leaky(h, c)
            k_quant(h, c)

        def k_half(h, c):
            for t in range(T):
                k_mm(h, c, t)
                k_aff(h, c, t)

        for a in range(4):
            x_tile(a)
        w_inter("q", 0, 1, "V")
        w_inter("q", 0, 0, "S")
        x_tile(4)
        small()
        x_quant(0, 0)
        x_quant(0, 1)
        w_quant("q", 0, 1)
        w_quant("q", 0, 0)
        w_inter("k", 0, 1, "S")
        w_inter("k", 0, 0, "V")
        load_w("q", 1)
        load_w("k", 1)
        for i in range(7):
            load_e(0, i)
        for t in range(T):
            q_mm(0, 0, t)
            q_sq(0, 0, t)
            q_aff(0, 0, t)
        w_quant("k", 0, 0)
        w_quant("k", 0, 1)
        k_half(0, 0)
        for a in range(5, A):
            x_tile(a)
        q_sums(0, 0)
        k_finish(0, 0)
        x_quant(1, 0)
        x_quant(1, 1)
        k_half(0, 1)
        q_root(0, 0)
        q_finish(0, 0)
        for t in range(T):
            q_mm(0, 1, t)
            q_sq(0, 1, t)
            q_aff(0, 1, t)
            if t:
                q_sum(0, 1, t - 1)
        k_finish(0, 1)
        q_sum(0, 1, T - 1)
        s_mm(0, 0)
        s_mm(0, 1)
        q_root(0, 1)
        s_max(0, 0)
        s_leaky(0, 0)
        def q_half(h, c):
            for t in range(T):
                q_mm(h, c, t)
                q_sq(h, c, t)
                q_aff(h, c, t)
                if t:
                    q_sum(h, c, t - 1)
            q_sum(h, c, T - 1)

        extra = {
            0: [lambda: w_inter("q", 1, 0, "S"), lambda: w_inter("q", 1, 1, "S"), lambda: q_finish(0, 1)],
            1: [lambda: w_quant("q", 1, 0), lambda: w_quant("q", 1, 1), lambda: q_half(1, 0)],
            2: [lambda: q_half(1, 1), lambda: q_root(1, 0), lambda: q_root(1, 1)],
            3: [lambda: w_inter("k", 1, 0, "S"), lambda: w_inter("k", 1, 1, "S"), lambda: q_finish(1, 0)],
            4: [lambda: w_quant("k", 1, 0), lambda: w_quant("k", 1, 1), lambda: k_half(1, 0), lambda: k_half(1, 1)],
            5: [lambda: k_finish(1, 0), lambda: k_finish(1, 1)],
            6: [],
            7: [lambda: q_finish(1, 1)],
        }
        order = [(h, i) for h in range(H) for i in range(A)]
        s_max(0, 1)
        s_leaky(0, 1)
        s_mm(0, 2)
        for n, (h, i) in enumerate(order):
            s_exp(h, i)
            if h == 0:
                for f in extra[i]:
                    f()
            if n + 2 < len(order):
                s_max(*order[n + 2])
                s_leaky(*order[n + 2])
            if n + 3 < len(order):
                s_mm(*order[n + 3])
            s_edge(h, i)
            if h == 1:
                c_fac(i)
                c_scale(i)
                if i > 0:
                    c_add(i - 1)
        c_add(A - 1)
